import numpy as np
import ml_dtypes


def mxq(x, axis, fmt="e4m3"):
    dtype, down = {"e4m3": (ml_dtypes.float8_e4m3fn, 7), "e5m2": (ml_dtypes.float8_e5m2, 14)}[fmt]
    v = np.moveaxis(np.asarray(x, np.float32).astype(ml_dtypes.bfloat16).astype(np.float64), axis, -1)
    blocks = v.reshape(v.shape[:-1] + (-1, 32))
    amax = np.abs(blocks).max(-1, keepdims=True)
    byte = np.maximum(np.where(amax > 0, np.frexp(amax)[1] - 1 + 127, 0) - down, 1)
    scale = np.exp2(byte - 127.0)
    codes = (blocks / scale).astype(np.float32).astype(dtype).astype(np.float64)
    return np.moveaxis((codes * scale).reshape(v.shape), -1, axis)


WIDE = False


def mx_kscale(k):
    if not WIDE:
        return np.ones(k)
    levels = np.array([10, -10, 5, -5, 0])
    if k % 512:
        return np.exp2(np.random.permutation(np.resize(levels, k // 32))).repeat(32)
    a = np.empty((k // 512, 16))
    for p in range(k // 512):
        a[p, :8] = np.random.permutation(np.resize(levels, 8))
        for g in range(8):
            far = levels[np.abs(levels - a[p, g]) >= 10]
            a[p, g + 8] = far[np.random.randint(len(far))]
    return np.exp2(a.ravel()).repeat(32)


def f64(x):
    return np.asarray(x).astype(np.float64)


def striped(idx):
    return np.tile(idx.reshape(-1, 16).T, (8, 1)).astype(np.uint16)


def unstriped(offs):
    return offs[:16].T.reshape(-1).astype(np.int64)


def striped8(idx):
    return np.concatenate([x.reshape(-1, 16).T for x in idx]).astype(np.uint16)


def runs(offs, k):
    lists = np.stack([offs[16 * r : 16 * r + 16].T.reshape(-1) for r in range(8)]).astype(np.int64)
    return lists[np.arange(k) % 512 // 64]


def pack_weight(w):
    k, n = w.shape
    w = f64(np.asarray(w, np.float32).astype(ml_dtypes.bfloat16)).reshape(k // 32, 32, n)
    amax = np.abs(w).max(1)
    byte = np.clip(np.where(amax > 0, np.frexp(amax)[1] - 1 + 127 - 7, 1), 1, 254)
    scaled = (w * np.exp2(127.0 - byte)[:, None, :]).reshape(k, n).astype(np.float32)
    words = np.ascontiguousarray(scaled.reshape(k // 512, 128, 4, n).transpose(0, 1, 3, 2)).astype(ml_dtypes.float8_e4m3fn).view(np.uint8)
    return words, np.ascontiguousarray(byte.astype(np.uint8).reshape(k // 512, 16, n))


def unpack_weight(words, scales):
    g, p, n, _ = words.shape
    vals = np.ascontiguousarray(words).view(ml_dtypes.float8_e4m3fn).astype(np.float64) * np.repeat(np.exp2(scales.astype(np.float64) - 127.0), 8, axis=1)[..., None]
    return vals.transpose(0, 1, 3, 2).reshape(g * 512, n)


def sigmoid(v):
    return 1.0 / (1.0 + np.exp(-np.maximum(v, -700.0)))


K, T, S, N, G, H, W = 512, 1024, 256, 512, 2048, 512, 128


def setup_inputs():
    n = np.random.standard_normal
    s = mx_kscale(K)[:, None]
    u = mx_kscale(K)
    packed_xT = pack_weight(n((K, T)) * s)
    packed_dT = pack_weight(n((K, G)) / s)
    perm = np.random.permutation(S)
    return {
        "x_words": packed_xT[0],
        "x_scales": packed_xT[1],
        "d_words": packed_dT[0],
        "d_scales": packed_dT[1],
        "sl": np.random.uniform(1.0, 2.0, (H, 1)).astype(np.float32),
        "th": (0.5 * n((H, 1))).astype(np.float32),
        "gn": (np.random.uniform(0.5, 1.5, (H, 1)) * u[:, None]).astype(np.float32),
        "w1": (n((H, N)) / np.sqrt(H) / u[:, None]).astype(np.float32),
        "offs": striped8(np.random.randint(0, T, (8, S))),
        "ka": striped8(np.random.randint(0, G, (8, H))),
        "kb": striped8(np.random.randint(0, G, (8, H))),
        "n1": striped(np.random.permutation(S)),
        "n2": striped(perm[:W]),
        "n3": striped(perm[W:]),
        "n4": striped(np.random.permutation(S)),
    }


def reference(x_words, x_scales, d_words, d_scales, sl, th, gn, w1, offs, ka, kb, n1, n2, n3, n4):
    d_ka = unpack_weight(d_words, d_scales)[np.arange(K)[:, None], runs(ka, K)]
    xq = unpack_weight(x_words, x_scales)[np.arange(K)[:, None], runs(offs, K)]
    d_kb = unpack_weight(d_words, d_scales)[np.arange(K)[:, None], runs(kb, K)]
    h = 0.0625 * (d_ka.T @ xq + d_kb.T @ xq)
    sg = sigmoid(f64(sl) * (h[:, unstriped(n1)] - f64(th)))
    z = f64(gn) * (h * sg)
    h2 = mxq(f64(w1), 0, "e4m3").T @ mxq(z, 0, "e4m3")
    pa = h2[:, unstriped(n2)]
    pb = h2[:, unstriped(n3)]
    rb = np.minimum(pa, pb)
    ra = np.maximum(pa, pb)
    ds = np.zeros((N, S))
    ds[:, unstriped(n2)] = ra
    dt = ds.copy()
    dt[:, unstriped(n3)] = rb
    return dt - dt[:, unstriped(n4)]

@@ -1,0 +1,239 @@
+from contextlib import ExitStack
+
+import concourse.mybir as mybir
+from concourse.masks import make_identity
+
+K, T, S, N, G, H, W = 512, 1024, 256, 512, 2048, 512, 128
+FLOPS = 2 * (2 * K * H * S) + 2 * H * N * S
+
+F32 = mybir.dt.float32
+BF16 = mybir.dt.bfloat16
+I32 = mybir.dt.int32
+U32 = mybir.dt.uint32
+U16 = mybir.dt.uint16
+U8 = mybir.dt.uint8
+FP8X4 = mybir.dt.float8_e4m3fn_x4
+ALU = mybir.AluOpType
+ACT = mybir.ActivationFunctionType
+
+P = 128
+PACK = 4
+HALF = S // 2
+LIST_ROWS = 16
+
+
+def tile_picked_haqesaordd_none_p_kernel(
+    tc, x_words, x_scales, d_words, d_scales, sl, th, gn, w1, offs, ka, kb, n1, n2, n3, n4, out
+):
+    nc = tc.nc
+    with ExitStack() as ctx:
+        pool = ctx.enter_context(tc.tile_pool(name="pool", bufs=1))
+        psum = ctx.enter_context(tc.psum_pool(name="psum", bufs=1))
+
+        def sb(name, shape, dtype):
+            return pool.tile(shape, dtype, name=name, align_bytes=64)
+
+        def load_list(name, src):
+            tile = sb(name, list(src.shape), U16)
+            nc.sync.dma_start(tile[:], src)
+            return tile
+
+        def load_scale_table(name, src, cols):
+            tile = sb(name, [P, cols], U8)
+            rows = src[0].bitcast(I32).unsqueeze(1).broadcast_to([16, 8, cols // 4])
+            nc.sync.dma_start(tile[:].bitcast(I32), rows)
+            return tile
+
+        def load_word_table(name, src, cols):
+            tile = sb(name, [P, cols], U32)
+            nc.sync.dma_start(tile[:].bitcast(I32), src[0].rearrange("p c r -> p (c r)").bitcast(I32))
+            return tile
+
+        offs_l = load_list("offs_l", offs)
+        x_sc = load_scale_table("x_sc", x_scales, T)
+        ka_l = load_list("ka_l", ka)
+        d_sc = load_scale_table("d_sc", d_scales, G)
+        kb_l = load_list("kb_l", kb)
+        x_wd = load_word_table("x_wd", x_words, T)
+        d_wd = load_word_table("d_wd", d_words, G)
+        n1_l = load_list("n1_l", n1)
+        n2_l = load_list("n2_l", n2)
+        n3_l = load_list("n3_l", n3)
+        n4_l = load_list("n4_l", n4)
+        w_raw = sb("w_raw", [P, PACK, N], F32)
+        for t in range(PACK):
+            nc.sync.dma_start(w_raw[:, t, :], w1.rearrange("(b t a) n -> t b a n", t=PACK, a=8)[t])
+
+        rows = sb("rows", [P, P], F32)
+        nc.gpsimd.memset(rows[:], 0.0)
+        for v, src in enumerate((sl, th, gn)):
+            nc.gpsimd.dma_start(
+                rows[v * PACK : (v + 1) * PACK, :].rearrange("t (b a) -> t b a", a=8),
+                src.rearrange("(b t a) o -> t b (a o)", t=PACK, a=8),
+            )
+        ident = sb("ident", [P, P], F32)
+        make_identity(nc, ident[:])
+        turned = psum.tile([P, P], F32, name="turned", tag="late23")
+        nc.tensor.transpose(turned[:], rows[:], ident[:])
+        vecs = sb("vecs", [P, 3 * PACK], F32)
+        nc.scalar.copy(vecs[:], turned[:, 0 : 3 * PACK])
+        sl_t, th_t, gn_t = (vecs[:, v * PACK : (v + 1) * PACK] for v in range(3))
+
+        slth = sb("slth", [P, PACK], F32)
+        bias = sb("bias", [P, PACK], F32)
+        nc.gpsimd.tensor_tensor(slth[:], sl_t, th_t, ALU.mult)
+        nc.gpsimd.tensor_scalar(bias[:], slth[:], -1.0, 0.0, ALU.mult, ALU.add)
+
+        planes = sb("planes", [P, 2 * H + S], U8)
+        nc.vector.memset(planes[:].bitcast(I32), 0)
+
+        picked_sc = sb("picked_sc", [P, 2 * H + S], U8)
+        nc.vector.tensor_copy(picked_sc[:, 2 * H :], x_sc[:].indirect(offs_l[:]))
+        nc.vector.tensor_copy(picked_sc[:, 0:H], d_sc[:].indirect(ka_l[:]))
+        nc.vector.tensor_copy(picked_sc[:, H : 2 * H], d_sc[:].indirect(kb_l[:]))
+        dealt_sc = sb("dealt_sc", [P, 2 * H + S], U8)
+        nc.vector.tensor_copy(dealt_sc[:, 2 * H :].bitcast(I32), picked_sc[:, 2 * H :].bitcast(I32))
+        nc.vector.tensor_copy(
+            dealt_sc[:, 0 : 2 * H].bitcast(I32).rearrange("p (g t b a) -> p g t b a", g=2, t=PACK, a=2),
+            picked_sc[:, 0 : 2 * H].bitcast(I32).rearrange("p (g b t a) -> p g t b a", g=2, t=PACK, a=2),
+        )
+        for s in range(4):
+            nc.scalar.dma_start(planes[s:P:32, :].bitcast(I32), dealt_sc[8 * s : P : 32, :].bitcast(I32))
+
+        xq = sb("xq", [P, S], U32)
+        nc.vector.tensor_copy(xq[:], x_wd[:].indirect(offs_l[:]))
+        dealt_wd = []
+        for g, lst in enumerate((ka_l, kb_l)):
+            picked = sb("picked_wd%d" % g, [P, H], U32)
+            nc.vector.tensor_copy(picked[:], d_wd[:].indirect(lst[:]))
+            dealt = sb("dealt_wd%d" % g, [P, PACK, P], U32)
+            src = picked[:].bitcast(I32).rearrange("p (b t a) -> p t b a", t=PACK, a=8)
+            if g == 0:
+                nc.vector.tensor_copy(dealt[:].bitcast(I32).rearrange("p t (b a) -> p t b a", a=8), src)
+            else:
+                for t in range(PACK):
+                    nc.vector.tensor_copy(dealt[:, t, :].bitcast(I32).rearrange("p (b a) -> p b a", a=8), src[:, t])
+            dealt_wd.append(dealt)
+
+        def quantise_w(c, engine_copy, tag):
+            grouped = pool.tile([P, N // 2, PACK], BF16, name="w_bf%d" % c, tag=tag, align_bytes=64)
+            engine_copy(
+                grouped[:].rearrange("p (c i) t -> p c t i", i=4),
+                w_raw[:, :, c * (N // 2) : (c + 1) * (N // 2)].rearrange("p t (c i) -> p c t i", i=4),
+            )
+            codes = sb("w_codes%d" % c, [P, N // 2], U32)
+            scales = sb("w_sc%d" % c, [P, N // 2], U8)
+            nc.vector.quantize_mx(codes[:].bitcast(FP8X4), scales[:], grouped[:].rearrange("p n t -> p (n t)"))
+            return codes, scales
+
+        w_lo = quantise_w(0, nc.scalar.copy, "w_bf0")
+
+        acc = [psum.tile([P, S], F32, name="acc%d" % t) for t in range(PACK)]
+        for g in range(2):
+            for t in range(PACK):
+                nc.tensor.matmul_mx(
+                    out=acc[t][:],
+                    lhsT=dealt_wd[g][:, t, :].bitcast(FP8X4),
+                    lhsT_scale=planes[:, g * H + t * P : g * H + (t + 1) * P],
+                    rhs=xq[:].bitcast(FP8X4),
+                    rhs_scale=planes[:, 2 * H :],
+                    start=(g == 0),
+                    stop=(g == 1),
+                )
+        h = []
+        for t in range(PACK):
+            tile = sb("h%d" % t, [P, S], F32)
+            if t == 0:
+                nc.scalar.activation(tile[:], acc[t][:], ACT.Copy, scale=0.0625)
+            else:
+                nc.vector.tensor_scalar(tile[:], acc[t][:], 0.0625, None, ALU.mult)
+            h.append(tile)
+
+        h2 = [sb("h2_%d" % m, [P, S], F32) for m in range(4)]
+        early = psum.tile([P, 2, HALF], F32, name="early")
+        late = [psum.tile([P, HALF], F32, name="late0"), psum.tile([P, HALF], F32, name="late1")]
+        z_codes = sb("z_codes", [P, S], U32)
+        z_sc = sb("z_sc", [P, S], U8)
+
+        def second_product(dst, weights, m, cols):
+            wcols = slice(m * P, (m + 1) * P)
+            nc.tensor.matmul_mx(
+                out=dst,
+                lhsT=weights[0][:, wcols].bitcast(FP8X4),
+                lhsT_scale=weights[1][:, wcols],
+                rhs=z_codes[:, cols].bitcast(FP8X4),
+                rhs_scale=z_sc[:, cols],
+                start=True,
+                stop=True,
+            )
+
+        for u in range(2):
+            cols = slice(u * HALF, (u + 1) * HALF)
+            lcols = slice(u * HALF // LIST_ROWS, (u + 1) * HALF // LIST_ROWS)
+            z_rows = sb("z_rows%d" % u, [P, PACK, HALF], BF16)
+            for t in range(PACK):
+                sg = sb("sg%d_%d" % (u, t), [P, HALF], F32)
+                nc.scalar.activation(
+                    sg[:], h[t][:].indirect(n1_l[:, lcols]), ACT.Sigmoid, scale=sl_t[:, t : t + 1], bias=bias[:, t : t + 1]
+                )
+                nc.vector.scalar_tensor_tensor(z_rows[:, t, :], h[t][:, cols], gn_t[:, t : t + 1], sg[:], ALU.mult, ALU.mult)
+            z_bf = sb("z_bf%d" % u, [P, HALF, PACK], BF16)
+            nc.vector.tensor_copy(
+                z_bf[:].rearrange("p (c i) t -> p c t i", i=4),
+                z_rows[:].rearrange("p t (c i) -> p c t i", i=4),
+            )
+            nc.vector.quantize_mx(z_codes[:, cols].bitcast(FP8X4), z_sc[:, cols], z_bf[:].rearrange("p n t -> p (n t)"))
+            for m in range(2):
+                second_product(early[:, m, :] if u == 0 else late[m][:], w_lo, m, cols)
+        for m in range(2):
+            nc.scalar.copy(h2[m][:, 0:HALF], early[:, m, :])
+        nc.scalar.copy(h2[0][:, HALF:], late[0][:])
+        nc.vector.tensor_copy(h2[1][:, HALF:], late[1][:])
+
+        w_hi = quantise_w(1, nc.vector.tensor_copy, "z_bf1")
+        late23 = psum.tile([P, 2, S], F32, name="late23", tag="late23")
+        for m in range(2):
+            second_product(late23[:, m, :], w_hi, m, slice(0, S))
+        for m in range(2):
+            nc.vector.tensor_copy(h2[2 + m][:], late23[:, m, :])
+
+        pair = [sb("pair%d" % m, [P, 2, W], F32) for m in range(4)]
+        ra = [sb("ra%d" % m, [P, W], F32) for m in range(4)]
+        rb = [sb("rb%d" % m, [P, W], F32) for m in range(4)]
+        dt = [sb("dt%d" % m, [P, S], F32) for m in range(4)]
+
+        def fetch_pairs(m):
+            nc.scalar.activation(pair[m][:, 0, :], h2[m][:].indirect(n2_l[:]), ACT.Copy)
+            nc.scalar.activation(pair[m][:, 1, :], h2[m][:].indirect(n3_l[:]), ACT.Copy)
+            nc.vector.tensor_tensor(ra[m][:], pair[m][:, 0, :], pair[m][:, 1, :], ALU.max)
+            nc.vector.tensor_tensor(rb[m][:], pair[m][:, 0, :], pair[m][:, 1, :], ALU.min)
+
+        def put_back(ms):
+            for m in ms:
+                nc.scalar.activation(dt[m][:].indirect(n2_l[:]), ra[m][:], ACT.Copy)
+            for m in ms:
+                nc.scalar.activation(dt[m][:].indirect(n3_l[:]), rb[m][:], ACT.Copy)
+
+        def finish(m):
+            res = sb("res%d" % m, [P, S], F32)
+            for u in range(2):
+                cols = slice(u * HALF, (u + 1) * HALF)
+                lcols = slice(u * HALF // LIST_ROWS, (u + 1) * HALF // LIST_ROWS)
+                other = sb("other%d_%d" % (m, u), [P, HALF], F32)
+                nc.scalar.activation(other[:], dt[m][:].indirect(n4_l[:, lcols]), ACT.Copy)
+                nc.vector.tensor_tensor(res[:, cols], dt[m][:, cols], other[:], ALU.subtract)
+                if m == 3:
+                    nc.sync.dma_start(out[m * P : (m + 1) * P, cols], res[:, cols])
+            if m < 3:
+                nc.sync.dma_start(out[m * P : (m + 1) * P, :], res[:])
+
+        fetch_pairs(0)
+        fetch_pairs(1)
+        put_back((0, 1))
+        finish(0)
+        fetch_pairs(2)
+        fetch_pairs(3)
+        finish(1)
+        put_back((2, 3))
+        finish(2)
+        finish(3)

@@ -49,28 +49,42 @@ def tile_picked_haqesaordd_none_p_kernel(
             nc.sync.dma_start(tile[:].bitcast(I32), src[0].rearrange("p c r -> p (c r)").bitcast(I32))
             return tile
 
+        def load_w(c, tag):
+            tile = pool.tile([P, PACK, N // 2], F32, name="w_raw%d" % c, tag=tag, align_bytes=64)
+            for t in range(PACK):
+                slot = w1.rearrange("(b t a) n -> t b a n", t=PACK, a=8)[t]
+                nc.sync.dma_start(tile[:, t, :], slot[:, :, c * (N // 2) : (c + 1) * (N // 2)])
+            return tile
+
+        rows = sb("rows", [P, P], F32)
+        nc.gpsimd.memset(rows[:], 0.0)
+
+        def load_row(v, src):
+            nc.sync.dma_start(
+                rows[v * PACK : (v + 1) * PACK, :].rearrange("t (b a) -> t b a", a=8),
+                src.rearrange("(b t a) o -> t b (a o)", t=PACK, a=8),
+            )
+
         offs_l = load_list("offs_l", offs)
         x_sc = load_scale_table("x_sc", x_scales, T)
         ka_l = load_list("ka_l", ka)
         d_sc = load_scale_table("d_sc", d_scales, G)
         kb_l = load_list("kb_l", kb)
-        x_wd = load_word_table("x_wd", x_words, T)
+        load_row(0, sl)
+        load_row(1, th)
         d_wd = load_word_table("d_wd", d_words, G)
+        load_row(2, gn)
         n1_l = load_list("n1_l", n1)
         n2_l = load_list("n2_l", n2)
+        x_wd = load_word_table("x_wd", x_words, T)
         n3_l = load_list("n3_l", n3)
         n4_l = load_list("n4_l", n4)
-        w_raw = sb("w_raw", [P, PACK, N], F32)
-        for t in range(PACK):
-            nc.sync.dma_start(w_raw[:, t, :], w1.rearrange("(b t a) n -> t b a n", t=PACK, a=8)[t])
 
-        rows = sb("rows", [P, P], F32)
-        nc.gpsimd.memset(rows[:], 0.0)
-        for v, src in enumerate((sl, th, gn)):
-            nc.gpsimd.dma_start(
-                rows[v * PACK : (v + 1) * PACK, :].rearrange("t (b a) -> t b a", a=8),
-                src.rearrange("(b t a) o -> t b (a o)", t=PACK, a=8),
-            )
+        warm_in = sb("warm_in", [P, 1], F32)
+        warm = sb("warm", [P, 1], F32)
+        nc.vector.memset(warm_in[:], 0.0)
+        nc.scalar.activation(warm[:], warm_in[:], ACT.Sigmoid)
+
         ident = sb("ident", [P, P], F32)
         make_identity(nc, ident[:])
         turned = psum.tile([P, P], F32, name="turned", tag="late23")
@@ -78,55 +92,67 @@ def tile_picked_haqesaordd_none_p_kernel(
         vecs = sb("vecs", [P, 3 * PACK], F32)
         nc.scalar.copy(vecs[:], turned[:, 0 : 3 * PACK])
         sl_t, th_t, gn_t = (vecs[:, v * PACK : (v + 1) * PACK] for v in range(3))
-
-        slth = sb("slth", [P, PACK], F32)
+        neg_sl = sb("neg_sl", [P, PACK], F32)
         bias = sb("bias", [P, PACK], F32)
-        nc.gpsimd.tensor_tensor(slth[:], sl_t, th_t, ALU.mult)
-        nc.gpsimd.tensor_scalar(bias[:], slth[:], -1.0, 0.0, ALU.mult, ALU.add)
-
-        planes = sb("planes", [P, 2 * H + S], U8)
-        nc.vector.memset(planes[:].bitcast(I32), 0)
+        nc.scalar.activation(neg_sl[:], sl_t, ACT.Copy, scale=-1.0)
+        for t in range(PACK):
+            nc.scalar.activation(bias[:, t : t + 1], th_t[:, t : t + 1], ACT.Copy, scale=neg_sl[:, t : t + 1])
 
         picked_sc = sb("picked_sc", [P, 2 * H + S], U8)
         nc.vector.tensor_copy(picked_sc[:, 2 * H :], x_sc[:].indirect(offs_l[:]))
         nc.vector.tensor_copy(picked_sc[:, 0:H], d_sc[:].indirect(ka_l[:]))
         nc.vector.tensor_copy(picked_sc[:, H : 2 * H], d_sc[:].indirect(kb_l[:]))
-        dealt_sc = sb("dealt_sc", [P, 2 * H + S], U8)
-        nc.vector.tensor_copy(dealt_sc[:, 2 * H :].bitcast(I32), picked_sc[:, 2 * H :].bitcast(I32))
-        nc.vector.tensor_copy(
-            dealt_sc[:, 0 : 2 * H].bitcast(I32).rearrange("p (g t b a) -> p g t b a", g=2, t=PACK, a=2),
-            picked_sc[:, 0 : 2 * H].bitcast(I32).rearrange("p (g b t a) -> p g t b a", g=2, t=PACK, a=2),
-        )
-        for s in range(4):
-            nc.scalar.dma_start(planes[s:P:32, :].bitcast(I32), dealt_sc[8 * s : P : 32, :].bitcast(I32))
+        planes = sb("planes", [P, 2 * H + S], U8)
+        nc.vector.tensor_copy(planes[:, 2 * H :].bitcast(I32), picked_sc[:, 2 * H :].bitcast(I32))
+        for g in range(2):
+            nc.vector.tensor_copy(
+                planes[:, g * H : (g + 1) * H].bitcast(I32).rearrange("p (t b a) -> p t b a", t=PACK, a=2),
+                picked_sc[:, g * H : (g + 1) * H].bitcast(I32).rearrange("p (b t a) -> p t b a", t=PACK, a=2),
+            )
+        for s in range(1, 4):
+            nc.sync.dma_start(planes[s:P:32, :].bitcast(I32), planes[8 * s : P : 32, :].bitcast(I32))
+        w_raw_lo = load_w(0, "picked_sc")
 
+
+        def pick_words(name, tag, offsets):
+            tile = pool.tile([P, offsets.shape[1] * LIST_ROWS], U32, name=name, tag=tag, align_bytes=64)
+            nc.vector.tensor_copy(tile[:], d_wd[:].indirect(offsets))
+            return tile
+
+        def deal_words(dst, picked):
+            nc.vector.tensor_copy(
+                dst.bitcast(I32).rearrange("p t (b a) -> p t b a", a=8),
+                picked.bitcast(I32).rearrange("p (b t a) -> p t b a", t=PACK, a=8),
+            )
+
+        half_list = H // 2 // LIST_ROWS
+        picked_a = pick_words("picked_a", "picked_wd0", ka_l[:])
         xq = sb("xq", [P, S], U32)
         nc.vector.tensor_copy(xq[:], x_wd[:].indirect(offs_l[:]))
-        dealt_wd = []
-        for g, lst in enumerate((ka_l, kb_l)):
-            picked = sb("picked_wd%d" % g, [P, H], U32)
-            nc.vector.tensor_copy(picked[:], d_wd[:].indirect(lst[:]))
-            dealt = sb("dealt_wd%d" % g, [P, PACK, P], U32)
-            src = picked[:].bitcast(I32).rearrange("p (b t a) -> p t b a", t=PACK, a=8)
-            if g == 0:
-                nc.vector.tensor_copy(dealt[:].bitcast(I32).rearrange("p t (b a) -> p t b a", a=8), src)
-            else:
-                for t in range(PACK):
-                    nc.vector.tensor_copy(dealt[:, t, :].bitcast(I32).rearrange("p (b a) -> p b a", a=8), src[:, t])
-            dealt_wd.append(dealt)
+        dealt_wd = [pool.tile([P, PACK, P], U32, name="dealt_a", tag="x_wd", align_bytes=64), sb("dealt_b", [P, PACK, P], U32)]
+        deal_words(dealt_wd[0][:], picked_a[:])
+        picked_b = pool.tile([P, H], U32, name="picked_b", tag="picked_wd0", align_bytes=64)
+        for u in range(2):
+            nc.vector.tensor_copy(
+                picked_b[:, u * H // 2 : (u + 1) * H // 2], d_wd[:].indirect(kb_l[:, u * half_list : (u + 1) * half_list])
+            )
+        for u in range(2):
+            deal_words(dealt_wd[1][:, :, u * P // 2 : (u + 1) * P // 2], picked_b[:, u * H // 2 : (u + 1) * H // 2])
 
-        def quantise_w(c, engine_copy, tag):
+        w_raw_hi = load_w(1, "d_wd")
+
+        def quantise_w(c, raw, engine_copy, tag):
             grouped = pool.tile([P, N // 2, PACK], BF16, name="w_bf%d" % c, tag=tag, align_bytes=64)
             engine_copy(
                 grouped[:].rearrange("p (c i) t -> p c t i", i=4),
-                w_raw[:, :, c * (N // 2) : (c + 1) * (N // 2)].rearrange("p t (c i) -> p c t i", i=4),
+                raw[:].rearrange("p t (c i) -> p c t i", i=4),
             )
             codes = sb("w_codes%d" % c, [P, N // 2], U32)
             scales = sb("w_sc%d" % c, [P, N // 2], U8)
             nc.vector.quantize_mx(codes[:].bitcast(FP8X4), scales[:], grouped[:].rearrange("p n t -> p (n t)"))
             return codes, scales
 
-        w_lo = quantise_w(0, nc.scalar.copy, "w_bf0")
+        w_lo = quantise_w(0, w_raw_lo, nc.scalar.copy, "w_bf0")
 
         acc = [psum.tile([P, S], F32, name="acc%d" % t) for t in range(PACK)]
         for g in range(2):
@@ -143,13 +169,11 @@ def tile_picked_haqesaordd_none_p_kernel(
         h = []
         for t in range(PACK):
             tile = sb("h%d" % t, [P, S], F32)
-            if t == 0:
-                nc.scalar.activation(tile[:], acc[t][:], ACT.Copy, scale=0.0625)
-            else:
-                nc.vector.tensor_scalar(tile[:], acc[t][:], 0.0625, None, ALU.mult)
+            nc.vector.tensor_scalar(tile[:], acc[t][:], 0.0625, None, ALU.mult)
             h.append(tile)
 
         h2 = [sb("h2_%d" % m, [P, S], F32) for m in range(4)]
+        sg = pool.tile([P, PACK, S], F32, name="sg", tag="picked_sc", align_bytes=64)
         early = psum.tile([P, 2, HALF], F32, name="early")
         late = [psum.tile([P, HALF], F32, name="late0"), psum.tile([P, HALF], F32, name="late1")]
         z_codes = sb("z_codes", [P, S], U32)
@@ -172,11 +196,10 @@ def tile_picked_haqesaordd_none_p_kernel(
             lcols = slice(u * HALF // LIST_ROWS, (u + 1) * HALF // LIST_ROWS)
             z_rows = sb("z_rows%d" % u, [P, PACK, HALF], BF16)
             for t in range(PACK):
-                sg = sb("sg%d_%d" % (u, t), [P, HALF], F32)
                 nc.scalar.activation(
-                    sg[:], h[t][:].indirect(n1_l[:, lcols]), ACT.Sigmoid, scale=sl_t[:, t : t + 1], bias=bias[:, t : t + 1]
+                    sg[:, t, cols], h[t][:].indirect(n1_l[:, lcols]), ACT.Sigmoid, scale=sl_t[:, t : t + 1], bias=bias[:, t : t + 1]
                 )
-                nc.vector.scalar_tensor_tensor(z_rows[:, t, :], h[t][:, cols], gn_t[:, t : t + 1], sg[:], ALU.mult, ALU.mult)
+                nc.vector.scalar_tensor_tensor(z_rows[:, t, :], h[t][:, cols], gn_t[:, t : t + 1], sg[:, t, cols], ALU.mult, ALU.mult)
             z_bf = sb("z_bf%d" % u, [P, HALF, PACK], BF16)
             nc.vector.tensor_copy(
                 z_bf[:].rearrange("p (c i) t -> p c t i", i=4),
@@ -190,7 +213,7 @@ def tile_picked_haqesaordd_none_p_kernel(
         nc.scalar.copy(h2[0][:, HALF:], late[0][:])
         nc.vector.tensor_copy(h2[1][:, HALF:], late[1][:])
 
-        w_hi = quantise_w(1, nc.vector.tensor_copy, "z_bf1")
+        w_hi = quantise_w(1, w_raw_hi, nc.vector.tensor_copy, "z_bf1")
         late23 = psum.tile([P, 2, S], F32, name="late23", tag="late23")
         for m in range(2):
             second_product(late23[:, m, :], w_hi, m, slice(0, S))

from contextlib import ExitStack

import concourse.mybir as mybir
from concourse.masks import make_identity

K, T, S, N, G, H, W = 512, 1024, 256, 512, 2048, 512, 128
FLOPS = 2 * (2 * K * H * S) + 2 * H * N * S

F32 = mybir.dt.float32
BF16 = mybir.dt.bfloat16
I32 = mybir.dt.int32
U32 = mybir.dt.uint32
U16 = mybir.dt.uint16
U8 = mybir.dt.uint8
FP8X4 = mybir.dt.float8_e4m3fn_x4
ALU = mybir.AluOpType
ACT = mybir.ActivationFunctionType

P = 128
PACK = 4
HALF = S // 2
LIST_ROWS = 16


def tile_picked_haqesaordd_none_p_kernel(
    tc, x_words, x_scales, d_words, d_scales, sl, th, gn, w1, offs, ka, kb, n1, n2, n3, n4, out
):
    nc = tc.nc
    with ExitStack() as ctx:
        pool = ctx.enter_context(tc.tile_pool(name="pool", bufs=1))
        psum = ctx.enter_context(tc.psum_pool(name="psum", bufs=1))

        def sb(name, shape, dtype):
            return pool.tile(shape, dtype, name=name, align_bytes=64)

        def load_list(name, src):
            tile = sb(name, list(src.shape), U16)
            nc.sync.dma_start(tile[:], src)
            return tile

        def load_scale_table(name, src, cols):
            tile = sb(name, [P, cols], U8)
            rows = src[0].bitcast(I32).unsqueeze(1).broadcast_to([16, 8, cols // 4])
            nc.sync.dma_start(tile[:].bitcast(I32), rows)
            return tile

        def load_word_table(name, src, cols):
            tile = sb(name, [P, cols], U32)
            nc.sync.dma_start(tile[:].bitcast(I32), src[0].rearrange("p c r -> p (c r)").bitcast(I32))
            return tile

        def load_w(c, tag):
            tile = pool.tile([P, PACK, N // 2], F32, name="w_raw%d" % c, tag=tag, align_bytes=64)
            for t in range(PACK):
                slot = w1.rearrange("(b t a) n -> t b a n", t=PACK, a=8)[t]
                nc.sync.dma_start(tile[:, t, :], slot[:, :, c * (N // 2) : (c + 1) * (N // 2)])
            return tile

        rows = sb("rows", [P, P], F32)
        nc.gpsimd.memset(rows[:], 0.0)

        def load_row(v, src):
            nc.sync.dma_start(
                rows[v * PACK : (v + 1) * PACK, :].rearrange("t (b a) -> t b a", a=8),
                src.rearrange("(b t a) o -> t b (a o)", t=PACK, a=8),
            )

        offs_l = load_list("offs_l", offs)
        x_sc = load_scale_table("x_sc", x_scales, T)
        ka_l = load_list("ka_l", ka)
        d_sc = load_scale_table("d_sc", d_scales, G)
        kb_l = load_list("kb_l", kb)
        load_row(0, sl)
        load_row(1, th)
        d_wd = load_word_table("d_wd", d_words, G)
        load_row(2, gn)
        n1_l = load_list("n1_l", n1)
        n2_l = load_list("n2_l", n2)
        x_wd = load_word_table("x_wd", x_words, T)
        n3_l = load_list("n3_l", n3)
        n4_l = load_list("n4_l", n4)

        warm_in = sb("warm_in", [P, 1], F32)
        warm = sb("warm", [P, 1], F32)
        nc.vector.memset(warm_in[:], 0.0)
        nc.scalar.activation(warm[:], warm_in[:], ACT.Sigmoid)

        ident = sb("ident", [P, P], F32)
        make_identity(nc, ident[:])
        turned = psum.tile([P, P], F32, name="turned", tag="late23")
        nc.tensor.transpose(turned[:], rows[:], ident[:])
        vecs = sb("vecs", [P, 3 * PACK], F32)
        nc.scalar.copy(vecs[:], turned[:, 0 : 3 * PACK])
        sl_t, th_t, gn_t = (vecs[:, v * PACK : (v + 1) * PACK] for v in range(3))
        neg_sl = sb("neg_sl", [P, PACK], F32)
        bias = sb("bias", [P, PACK], F32)
        nc.scalar.activation(neg_sl[:], sl_t, ACT.Copy, scale=-1.0)
        for t in range(PACK):
            nc.scalar.activation(bias[:, t : t + 1], th_t[:, t : t + 1], ACT.Copy, scale=neg_sl[:, t : t + 1])

        picked_sc = sb("picked_sc", [P, 2 * H + S], U8)
        nc.vector.tensor_copy(picked_sc[:, 2 * H :], x_sc[:].indirect(offs_l[:]))
        nc.vector.tensor_copy(picked_sc[:, 0:H], d_sc[:].indirect(ka_l[:]))
        nc.vector.tensor_copy(picked_sc[:, H : 2 * H], d_sc[:].indirect(kb_l[:]))
        planes = sb("planes", [P, 2 * H + S], U8)
        nc.vector.tensor_copy(planes[:, 2 * H :].bitcast(I32), picked_sc[:, 2 * H :].bitcast(I32))
        for g in range(2):
            nc.vector.tensor_copy(
                planes[:, g * H : (g + 1) * H].bitcast(I32).rearrange("p (t b a) -> p t b a", t=PACK, a=2),
                picked_sc[:, g * H : (g + 1) * H].bitcast(I32).rearrange("p (b t a) -> p t b a", t=PACK, a=2),
            )
        for s in range(1, 4):
            nc.sync.dma_start(planes[s:P:32, :].bitcast(I32), planes[8 * s : P : 32, :].bitcast(I32))
        w_raw_lo = load_w(0, "picked_sc")


        def pick_words(name, tag, offsets):
            tile = pool.tile([P, offsets.shape[1] * LIST_ROWS], U32, name=name, tag=tag, align_bytes=64)
            nc.vector.tensor_copy(tile[:], d_wd[:].indirect(offsets))
            return tile

        def deal_words(dst, picked):
            nc.vector.tensor_copy(
                dst.bitcast(I32).rearrange("p t (b a) -> p t b a", a=8),
                picked.bitcast(I32).rearrange("p (b t a) -> p t b a", t=PACK, a=8),
            )

        half_list = H // 2 // LIST_ROWS
        picked_a = pick_words("picked_a", "picked_wd0", ka_l[:])
        xq = sb("xq", [P, S], U32)
        nc.vector.tensor_copy(xq[:], x_wd[:].indirect(offs_l[:]))
        dealt_wd = [pool.tile([P, PACK, P], U32, name="dealt_a", tag="x_wd", align_bytes=64), sb("dealt_b", [P, PACK, P], U32)]
        deal_words(dealt_wd[0][:], picked_a[:])
        picked_b = pool.tile([P, H], U32, name="picked_b", tag="picked_wd0", align_bytes=64)
        for u in range(2):
            nc.vector.tensor_copy(
                picked_b[:, u * H // 2 : (u + 1) * H // 2], d_wd[:].indirect(kb_l[:, u * half_list : (u + 1) * half_list])
            )
        for u in range(2):
            deal_words(dealt_wd[1][:, :, u * P // 2 : (u + 1) * P // 2], picked_b[:, u * H // 2 : (u + 1) * H // 2])

        w_raw_hi = load_w(1, "d_wd")

        def quantise_w(c, raw, engine_copy, tag):
            grouped = pool.tile([P, N // 2, PACK], BF16, name="w_bf%d" % c, tag=tag, align_bytes=64)
            engine_copy(
                grouped[:].rearrange("p (c i) t -> p c t i", i=4),
                raw[:].rearrange("p t (c i) -> p c t i", i=4),
            )
            codes = sb("w_codes%d" % c, [P, N // 2], U32)
            scales = sb("w_sc%d" % c, [P, N // 2], U8)
            nc.vector.quantize_mx(codes[:].bitcast(FP8X4), scales[:], grouped[:].rearrange("p n t -> p (n t)"))
            return codes, scales

        w_lo = quantise_w(0, w_raw_lo, nc.scalar.copy, "w_bf0")

        acc = [psum.tile([P, S], F32, name="acc%d" % t) for t in range(PACK)]
        for g in range(2):
            for t in range(PACK):
                nc.tensor.matmul_mx(
                    out=acc[t][:],
                    lhsT=dealt_wd[g][:, t, :].bitcast(FP8X4),
                    lhsT_scale=planes[:, g * H + t * P : g * H + (t + 1) * P],
                    rhs=xq[:].bitcast(FP8X4),
                    rhs_scale=planes[:, 2 * H :],
                    start=(g == 0),
                    stop=(g == 1),
                )
        h = []
        for t in range(PACK):
            tile = sb("h%d" % t, [P, S], F32)
            nc.vector.tensor_scalar(tile[:], acc[t][:], 0.0625, None, ALU.mult)
            h.append(tile)

        h2 = [sb("h2_%d" % m, [P, S], F32) for m in range(4)]
        sg = pool.tile([P, PACK, S], F32, name="sg", tag="picked_sc", align_bytes=64)
        early = psum.tile([P, 2, HALF], F32, name="early")
        late = [psum.tile([P, HALF], F32, name="late0"), psum.tile([P, HALF], F32, name="late1")]
        z_codes = sb("z_codes", [P, S], U32)
        z_sc = sb("z_sc", [P, S], U8)

        def second_product(dst, weights, m, cols):
            wcols = slice(m * P, (m + 1) * P)
            nc.tensor.matmul_mx(
                out=dst,
                lhsT=weights[0][:, wcols].bitcast(FP8X4),
                lhsT_scale=weights[1][:, wcols],
                rhs=z_codes[:, cols].bitcast(FP8X4),
                rhs_scale=z_sc[:, cols],
                start=True,
                stop=True,
            )

        for u in range(2):
            cols = slice(u * HALF, (u + 1) * HALF)
            lcols = slice(u * HALF // LIST_ROWS, (u + 1) * HALF // LIST_ROWS)
            z_rows = sb("z_rows%d" % u, [P, PACK, HALF], BF16)
            for t in range(PACK):
                nc.scalar.activation(
                    sg[:, t, cols], h[t][:].indirect(n1_l[:, lcols]), ACT.Sigmoid, scale=sl_t[:, t : t + 1], bias=bias[:, t : t + 1]
                )
                nc.vector.scalar_tensor_tensor(z_rows[:, t, :], h[t][:, cols], gn_t[:, t : t + 1], sg[:, t, cols], ALU.mult, ALU.mult)
            z_bf = sb("z_bf%d" % u, [P, HALF, PACK], BF16)
            nc.vector.tensor_copy(
                z_bf[:].rearrange("p (c i) t -> p c t i", i=4),
                z_rows[:].rearrange("p t (c i) -> p c t i", i=4),
            )
            nc.vector.quantize_mx(z_codes[:, cols].bitcast(FP8X4), z_sc[:, cols], z_bf[:].rearrange("p n t -> p (n t)"))
            for m in range(2):
                second_product(early[:, m, :] if u == 0 else late[m][:], w_lo, m, cols)
        for m in range(2):
            nc.scalar.copy(h2[m][:, 0:HALF], early[:, m, :])
        nc.scalar.copy(h2[0][:, HALF:], late[0][:])
        nc.vector.tensor_copy(h2[1][:, HALF:], late[1][:])

        w_hi = quantise_w(1, w_raw_hi, nc.vector.tensor_copy, "z_bf1")
        late23 = psum.tile([P, 2, S], F32, name="late23", tag="late23")
        for m in range(2):
            second_product(late23[:, m, :], w_hi, m, slice(0, S))
        for m in range(2):
            nc.vector.tensor_copy(h2[2 + m][:], late23[:, m, :])

        pair = [sb("pair%d" % m, [P, 2, W], F32) for m in range(4)]
        ra = [sb("ra%d" % m, [P, W], F32) for m in range(4)]
        rb = [sb("rb%d" % m, [P, W], F32) for m in range(4)]
        dt = [sb("dt%d" % m, [P, S], F32) for m in range(4)]

        def fetch_pairs(m):
            nc.scalar.activation(pair[m][:, 0, :], h2[m][:].indirect(n2_l[:]), ACT.Copy)
            nc.scalar.activation(pair[m][:, 1, :], h2[m][:].indirect(n3_l[:]), ACT.Copy)
            nc.vector.tensor_tensor(ra[m][:], pair[m][:, 0, :], pair[m][:, 1, :], ALU.max)
            nc.vector.tensor_tensor(rb[m][:], pair[m][:, 0, :], pair[m][:, 1, :], ALU.min)

        def put_back(ms):
            for m in ms:
                nc.scalar.activation(dt[m][:].indirect(n2_l[:]), ra[m][:], ACT.Copy)
            for m in ms:
                nc.scalar.activation(dt[m][:].indirect(n3_l[:]), rb[m][:], ACT.Copy)

        def finish(m):
            res = sb("res%d" % m, [P, S], F32)
            for u in range(2):
                cols = slice(u * HALF, (u + 1) * HALF)
                lcols = slice(u * HALF // LIST_ROWS, (u + 1) * HALF // LIST_ROWS)
                other = sb("other%d_%d" % (m, u), [P, HALF], F32)
                nc.scalar.activation(other[:], dt[m][:].indirect(n4_l[:, lcols]), ACT.Copy)
                nc.vector.tensor_tensor(res[:, cols], dt[m][:, cols], other[:], ALU.subtract)
                if m == 3:
                    nc.sync.dma_start(out[m * P : (m + 1) * P, cols], res[:, cols])
            if m < 3:
                nc.sync.dma_start(out[m * P : (m + 1) * P, :], res[:])

        fetch_pairs(0)
        fetch_pairs(1)
        put_back((0, 1))
        finish(0)
        fetch_pairs(2)
        fetch_pairs(3)
        finish(1)
        put_back((2, 3))
        finish(2)
        finish(3)
